import numpy as np
import ml_dtypes


def mxq(x, axis, fmt="e4m3"):
    dtype, down = {"e4m3": (ml_dtypes.float8_e4m3fn, 7), "e5m2": (ml_dtypes.float8_e5m2, 14)}[fmt]
    v = np.moveaxis(np.asarray(x, np.float32).astype(ml_dtypes.bfloat16).astype(np.float64), axis, -1)
    blocks = v.reshape(v.shape[:-1] + (-1, 32))
    amax = np.abs(blocks).max(-1, keepdims=True)
    byte = np.maximum(np.where(amax > 0, np.frexp(amax)[1] - 1 + 127, 0) - down, 1)
    scale = np.exp2(byte - 127.0)
    codes = (blocks / scale).astype(np.float32).astype(dtype).astype(np.float64)
    return np.moveaxis((codes * scale).reshape(v.shape), -1, axis)


WIDE = False


def mx_kscale(k):
    if not WIDE:
        return np.ones(k)
    levels = np.array([10, -10, 5, -5, 0])
    if k % 512:
        return np.exp2(np.random.permutation(np.resize(levels, k // 32))).repeat(32)
    a = np.empty((k // 512, 16))
    for p in range(k // 512):
        a[p, :8] = np.random.permutation(np.resize(levels, 8))
        for g in range(8):
            far = levels[np.abs(levels - a[p, g]) >= 10]
            a[p, g + 8] = far[np.random.randint(len(far))]
    return np.exp2(a.ravel()).repeat(32)


def f64(x):
    return np.asarray(x).astype(np.float64)


def striped(idx):
    return np.tile(idx.reshape(-1, 16).T, (8, 1)).astype(np.uint16)


def unstriped(offs):
    return offs[:16].T.reshape(-1).astype(np.int64)


def pack_weight(w):
    k, n = w.shape
    w = f64(np.asarray(w, np.float32).astype(ml_dtypes.bfloat16)).reshape(k // 32, 32, n)
    amax = np.abs(w).max(1)
    byte = np.clip(np.where(amax > 0, np.frexp(amax)[1] - 1 + 127 - 7, 1), 1, 254)
    scaled = (w * np.exp2(127.0 - byte)[:, None, :]).reshape(k, n).astype(np.float32)
    words = np.ascontiguousarray(scaled.reshape(k // 512, 128, 4, n).transpose(0, 1, 3, 2)).astype(ml_dtypes.float8_e4m3fn).view(np.uint8)
    return words, np.ascontiguousarray(byte.astype(np.uint8).reshape(k // 512, 16, n))


def unpack_weight(words, scales):
    g, p, n, _ = words.shape
    vals = np.ascontiguousarray(words).view(ml_dtypes.float8_e4m3fn).astype(np.float64) * np.repeat(np.exp2(scales.astype(np.float64) - 127.0), 8, axis=1)[..., None]
    return vals.transpose(0, 1, 3, 2).reshape(g * 512, n)


E2M1 = np.array([0.0, 0.5, 1.0, 1.5, 2.0, 3.0, 4.0, 6.0, -0.0, -0.5, -1.0, -1.5, -2.0, -3.0, -4.0, -6.0])


def pack_fp4(w):
    k, n = w.shape
    w = f64(np.asarray(w, np.float32).astype(ml_dtypes.bfloat16)).reshape(k // 32, 32, n)
    amax = np.abs(w).max(1)
    mant, ex = np.frexp(amax / 6.0)
    byte = np.clip(np.where(amax > 0, np.where(mant > 0.5, ex, ex - 1) + 127, 1), 1, 254)
    scaled = (w * np.exp2(127.0 - byte)[:, None, :]).reshape(k, n).astype(np.float32)
    c = np.ascontiguousarray(scaled.reshape(k // 512, 128, 4, n).transpose(0, 1, 3, 2)).astype(ml_dtypes.float4_e2m1fn).view(np.uint8) & 0xF
    words = (c[..., 0::2] | (c[..., 1::2] << 4)).reshape(k // 512, 128, 2 * n)
    return np.ascontiguousarray(words), np.ascontiguousarray(byte.astype(np.uint8).reshape(k // 512, 16, n))


def unpack_fp4(words, scales):
    g, _, n = scales.shape
    words = np.ascontiguousarray(words).reshape(g, 128, n, 2)
    nib = np.empty((g, 128, n, 4), np.uint8)
    nib[..., 0::2] = words & 0xF
    nib[..., 1::2] = words >> 4
    vals = E2M1[nib] * np.repeat(np.exp2(scales.astype(np.float64) - 127.0), 8, axis=1)[..., None]
    return vals.transpose(0, 1, 3, 2).reshape(g * 512, n)


K, T, S, D, N, H = 512, 2048, 512, 4, 256, 512


def setup_inputs():
    n = np.random.standard_normal
    s = mx_kscale(K)[:, None]
    u = mx_kscale(H)
    packed_xT = pack_weight(n((K, T)) * s)
    packed_w1 = pack_fp4(n((K, H)) / np.sqrt(K) / s)
    packed_w2 = pack_fp4(n((K, H)) / np.sqrt(K) / s)
    packed_w3 = pack_fp4(n((H, N)) / np.sqrt(H) / u[:, None])
    return {
        "x_words": packed_xT[0],
        "x_scales": packed_xT[1],
        "w1_words": packed_w1[0],
        "w1_scales": packed_w1[1],
        "w2_words": packed_w2[0],
        "w2_scales": packed_w2[1],
        "beta": (np.random.uniform(0.6, 1.2, (H, 1))).astype(np.float32),
        "unit": (np.random.uniform(0.6, 1.4, (H, 1)) * u[:, None]).astype(np.float32),
        "w3_words": packed_w3[0],
        "w3_scales": packed_w3[1],
        "offs": striped(np.random.permutation(T)[:S]),
        "nei": striped(np.random.permutation(S)),
    }


def reference(x_words, x_scales, w1_words, w1_scales, w2_words, w2_scales, beta, unit, w3_words, w3_scales, offs, nei):
    xq = unpack_weight(x_words, x_scales)[:, unstriped(offs)]
    un = unpack_fp4(w1_words, w1_scales).T @ xq
    sp = unpack_fp4(w2_words, w2_scales).T @ xq
    vel = f64(beta) * (np.log(np.exp(un) + 1.0)) - (0.7 * (np.log(np.exp(sp) + 1.0)))
    sn = sp[:, unstriped(nei)]
    dst = sn - sp
    cosn = (vel * dst) / (np.abs(vel) + np.abs(dst) + 0.3)
    prtop = cosn.reshape(len(cosn), -1, D).max(axis=2)
    prexp = np.exp(cosn - np.repeat(prtop, D, axis=1))
    prsum = prexp.reshape(len(prexp), -1, D).sum(axis=2)
    pr = prexp / np.repeat(prsum, D, axis=1)
    drft = pr * dst
    tot = drft.reshape(len(drft), -1, D).sum(axis=2)
    hid = f64(unit) * (np.repeat(tot, D, axis=1) * vel)
    return unpack_fp4(w3_words, w3_scales).T @ mxq(hid, 0, "e4m3")

@@ -1,0 +1,288 @@
+from contextlib import ExitStack
+
+import concourse.mybir as mybir
+from concourse.masks import make_identity
+
+K, T, S, D, N, H = 512, 2048, 512, 4, 256, 512
+FLOPS = 2 * K * H * S * 2 + 2 * H * N * S
+
+F32 = mybir.dt.float32
+BF16 = mybir.dt.bfloat16
+I32 = mybir.dt.int32
+U32 = mybir.dt.uint32
+U16 = mybir.dt.uint16
+U8 = mybir.dt.uint8
+FP8X4 = mybir.dt.float8_e4m3fn_x4
+FP4X4 = mybir.dt.float4_e2m1fn_x4
+ALU = mybir.AluOpType
+ACT = mybir.ActivationFunctionType
+
+P = 128
+PACK = 4
+CHUNKS = 4
+CW = S // CHUNKS
+GROUPS = CW // D
+DECAY = 0.7
+DEN_BIAS = 0.3
+LN_FLOOR = 2.0**-64
+
+
+def load_scale_rows(queues, plane, scales):
+    for q, queue in enumerate(queues):
+        queue.dma_start(out=plane[32 * q : 32 * q + 4, :].bitcast(I32), in_=scales[0, 4 * q : 4 * q + 4, :].bitcast(I32))
+
+
+def deal_columns(nc, pool, name, words, plane):
+    dealt_words = pool.tile([P, 2 * H], U8, name=name + "_dealt_words", align_bytes=64)
+    dealt_plane = pool.tile([P, H], U8, name=name + "_dealt_plane", align_bytes=64)
+    nc.vector.tensor_copy(
+        out=dealt_words[:].rearrange("p (t a m b) -> p a t m b", t=PACK, m=8, b=2),
+        in_=words[:].rearrange("p (a m t b) -> p a t m b", t=PACK, m=8, b=2),
+    )
+    nc.vector.tensor_copy(
+        out=dealt_plane[:].rearrange("p (t a m) -> p a t m", t=PACK, m=16),
+        in_=plane[:].rearrange("p (a m t) -> p a t m", t=PACK, m=16),
+    )
+    return dealt_words, dealt_plane
+
+
+def tile_picked_yrnavl_tot_p_kernel(
+    tc, x_words, x_scales, w1_words, w1_scales, w2_words, w2_scales, beta, unit, w3_words, w3_scales, offs, nei, out
+):
+    nc = tc.nc
+    with ExitStack() as ctx:
+        keep = ctx.enter_context(tc.tile_pool(name="keep", bufs=1))
+        ring = ctx.enter_context(tc.tile_pool(name="ring", bufs=4))
+        psum = ctx.enter_context(tc.psum_pool(name="psum", bufs=1))
+
+        def bank(b):
+            return psum.tile([P, 512], F32, name="bank%d" % b, tag="bank%d" % b)
+
+        x_plane = keep.tile([P, T], U8, name="x_plane", tag="x_plane", align_bytes=64)
+        w_plane = keep.tile([P, H], U8, name="w_plane", align_bytes=64)
+        w1_plane = keep.tile([P, H], U8, name="w1_plane", align_bytes=64)
+        nc.gpsimd.memset(x_plane[:].bitcast(I32), 0)
+        nc.gpsimd.memset(w_plane[:].bitcast(I32), 0)
+        nc.gpsimd.memset(w1_plane[:].bitcast(I32), 0)
+
+        x_table = keep.tile([P, T], I32, name="x_table", tag="x_table", align_bytes=64)
+        offs_sb = keep.tile([P, S // 16], U16, name="offs_sb")
+        nei_sb = keep.tile([P, S // 16], U16, name="nei_sb")
+        w_words = keep.tile([P, 2 * H], U8, name="w_words", align_bytes=64)
+        on_sync = [nc.sync] * 4
+
+        nc.sync.dma_start(offs_sb[:], offs)
+        nc.sync.dma_start(out=w_words[:].bitcast(I32), in_=w2_words[0].bitcast(I32))
+        load_scale_rows(on_sync, x_plane, x_scales)
+        nc.sync.dma_start(out=x_table[:], in_=x_words[0].rearrange("p n t -> p (n t)").bitcast(I32))
+        load_scale_rows([nc.sync, nc.sync, nc.sync, nc.gpsimd], w_plane, w2_scales)
+
+        ident = keep.tile([P, P], F32, name="ident")
+        make_identity(nc, ident[:])
+
+        x_codes = keep.tile([P, S], U32, name="x_codes", align_bytes=64)
+        x_picked_plane = keep.tile([P, S], U8, name="x_picked_plane", align_bytes=64)
+        w2_dealt, w2_dealt_plane = deal_columns(nc, keep, "w2", w_words, w_plane)
+        nc.vector.tensor_copy(x_picked_plane[:], x_plane[:].indirect(offs_sb[:]))
+        nc.vector.tensor_copy(x_codes[:], x_table[:].bitcast(U32).indirect(offs_sb[:]))
+
+        nc.sync.dma_start(out=w_words[:].bitcast(I32), in_=w1_words[0].bitcast(I32))
+        load_scale_rows(on_sync, w1_plane, w1_scales)
+        nc.sync.dma_start(nei_sb[:], nei)
+        w1_dealt, w1_dealt_plane = deal_columns(nc, keep, "w1", w_words, w1_plane)
+
+        beta_sb = keep.tile([P, PACK], F32, name="beta_sb", tag="x_table", align_bytes=64)
+        unit_sb = keep.tile([P, PACK], F32, name="unit_sb", tag="x_plane", align_bytes=64)
+        nc.sync.dma_start(out=beta_sb[:], in_=beta.rearrange("(p t) o -> p (t o)", t=PACK))
+        nc.sync.dma_start(out=unit_sb[:], in_=unit.rearrange("(p t) o -> p (t o)", t=PACK))
+        w3_sb = w_words[:, : 2 * N]
+        w3_plane = w_plane[:, :N]
+        nc.sync.dma_start(out=w3_sb.bitcast(I32), in_=w3_words[0].bitcast(I32))
+        load_scale_rows(on_sync, w3_plane, w3_scales)
+
+        rate = keep.tile([P, PACK], F32, name="rate")
+        gain = keep.tile([P, PACK], F32, name="gain")
+        nc.gpsimd.tensor_scalar(rate[:], beta_sb[:], -1.0 / DECAY, 0.0, ALU.mult, ALU.add)
+        nc.gpsimd.tensor_scalar(gain[:], unit_sb[:], DECAY, 0.0, ALU.mult, ALU.add)
+
+        def product(acc, words, plane, t):
+            nc.tensor.matmul_mx(
+                out=acc[:],
+                lhsT=words[:, 2 * P * t : 2 * P * (t + 1)].bitcast(FP4X4),
+                lhsT_scale=plane[:, P * t : P * (t + 1)],
+                rhs=x_codes[:].bitcast(FP8X4),
+                rhs_scale=x_picked_plane[:],
+                start=True,
+                stop=True,
+            )
+
+        def wide(name):
+            return keep.tile([P, CHUNKS, PACK, CW], F32, name=name)
+
+        def by_chunk(ap):
+            return ap.rearrange("p (c j) -> p c j", c=CHUNKS)
+
+        sp = [bank(t) for t in range(PACK)]
+        un = [bank(PACK + t) for t in range(PACK)]
+        for t in range(PACK):
+            product(sp[t], w2_dealt, w2_dealt_plane, t)
+        for t in range(PACK):
+            product(un[t], w1_dealt, w1_dealt_plane, t)
+
+        dst = wide("dst")
+        abs_dst = wide("abs_dst")
+        sig_sp = [keep.tile([P, S], F32, name="sig_sp%d" % t) for t in range(PACK)]
+        sig_un = [keep.tile([P, S], F32, name="sig_un%d" % t) for t in range(PACK)]
+        for t in range(PACK):
+            nc.scalar.activation(sig_sp[t][:], sp[t][:], ACT.Sigmoid, scale=-1.0)
+            window = keep.tile([P, S], F32, name="window%d" % t)
+            nc.scalar.copy(window[:], sp[t][:])
+            fetched = ring.tile([P, S], F32, name="fetched")
+            for h in range(2):
+                nc.vector.tensor_copy(fetched[:, 256 * h : 256 * (h + 1)], window[:].indirect(nei_sb[:, 16 * h : 16 * (h + 1)]))
+            nc.vector.tensor_tensor(dst[:, :, t, :], by_chunk(fetched[:]), by_chunk(window[:]), ALU.subtract)
+            if t in (0,):
+                nc.vector.scalar_tensor_tensor(abs_dst[:, :, t, :], dst[:, :, t, :], -1.0, dst[:, :, t, :], ALU.mult, ALU.max)
+        for t in range(PACK):
+            nc.scalar.activation(sig_un[t][:], un[t][:], ACT.Sigmoid, scale=-1.0)
+
+        vel = wide("vel")
+        log_den = wide("log_den")
+        for t in range(PACK):
+            log_sp = ring.tile([P, S], F32, name="log_sp")
+            log_un = ring.tile([P, S], F32, name="log_un")
+            nc.scalar.activation(log_sp[:], sig_sp[t][:], ACT.Ln, bias=LN_FLOOR)
+            nc.scalar.activation(log_un[:], sig_un[t][:], ACT.Ln, bias=LN_FLOOR)
+            soft_sp = ring.tile([P, S], F32, name="soft_sp")
+            soft_un = ring.tile([P, S], F32, name="soft_un")
+            nc.vector.scalar_tensor_tensor(soft_sp[:], sp[t][:], -1.0, log_sp[:], ALU.mult, ALU.min)
+            nc.vector.scalar_tensor_tensor(soft_un[:], un[t][:], -1.0, log_un[:], ALU.mult, ALU.min)
+            nc.vector.scalar_tensor_tensor(
+                vel[:, :, t, :], by_chunk(soft_un[:]), rate[:, t : t + 1], by_chunk(soft_sp[:]), ALU.mult, ALU.add
+            )
+            abs_vel = ring.tile([P, S], F32, name="abs_vel")
+            if t not in (0,):
+                nc.scalar.activation(abs_dst[:, :, t, :], dst[:, :, t, :], ACT.Abs)
+            nc.scalar.activation(by_chunk(abs_vel[:]), vel[:, :, t, :], ACT.Abs, scale=DECAY)
+            den = ring.tile([P, S], F32, name="den")
+            nc.vector.tensor_tensor(by_chunk(den[:]), by_chunk(abs_vel[:]), abs_dst[:, :, t, :], ALU.add)
+            nc.scalar.activation(log_den[:, :, t, :], by_chunk(den[:]), ACT.Ln, bias=DEN_BIAS)
+
+        def flat(ap):
+            return ap.rearrange("p t j -> p (t j)")
+
+        num = wide("num")
+        for c in range(CHUNKS):
+            nc.vector.tensor_tensor(flat(num[:, c]), flat(vel[:, c]), flat(dst[:, c]), ALU.mult)
+
+        stages = [dict() for c in range(CHUNKS)]
+        for c in range(CHUNKS):
+            dst_t = bank(c)
+            for d in range(D):
+                nc.tensor.transpose(dst_t[:, P * d : P * (d + 1)], flat(dst[:, c])[:, d :: D], ident[:])
+            stages[c]["dst_t"] = dst_t
+
+        def cosine(c):
+            st = stages[c]
+            inv_den = ring.tile([P, PACK * CW], F32, name="inv_den")
+            nc.scalar.activation(inv_den[:], flat(log_den[:, c]), ACT.Exp, scale=-1.0)
+            cosn = ring.tile([P, PACK * CW], F32, name="cosn")
+            nc.vector.tensor_tensor(cosn[:], flat(num[:, c]), inv_den[:], ALU.mult)
+            neg_top = ring.tile([P, P], F32, name="neg_top")
+            nc.vector.tensor_reduce(
+                neg_top[:], cosn[:].rearrange("p (g d) -> p g d", d=D), mybir.AxisListType.X, ALU.max, negate=True
+            )
+            shifted = bank(4 + c % 2)
+            for d in range(D):
+                nc.tensor.matmul(
+                    shifted[:, P * d : P * (d + 1)], cosn[:, d :: D], ident[:], start=(d == 0), stop=False, is_transpose=True
+                )
+            for d in range(D):
+                nc.tensor.matmul(
+                    shifted[:, P * d : P * (d + 1)], neg_top[:], ident[:], start=False, stop=(d == D - 1), is_transpose=True
+                )
+            st["shifted"] = shifted
+
+        def weights(c):
+            st = stages[c]
+            prexp = ring.tile([P, D * P], F32, name="prexp")
+            nc.scalar.activation(prexp[:], st["shifted"][:], ACT.Exp, scale=DECAY)
+            sums = bank(6 + c % 2)
+            exp_sum = sums[:, :P]
+            drift_sum = sums[:, P : 2 * P]
+
+            def add_up(total, terms):
+                for d in range(D):
+                    nc.tensor.matmul(
+                        total, terms[:, P * d : P * (d + 1)], ident[:], start=(d == 0), stop=(d == D - 1), is_transpose=True
+                    )
+
+            add_up(exp_sum, prexp)
+            upper = ring.tile([P, P // 2], F32, name="upper")
+            nc.scalar.copy(upper[:], exp_sum[:, P // 2 :])
+            partner = ring.tile([P, PACK, GROUPS], F32, name="partner")
+            for t in range(PACK):
+                other = (t + 2) % PACK
+                nc.scalar.activation(
+                    partner[:, t, :], exp_sum[:, GROUPS * other : GROUPS * (other + 1)], ACT.Copy, scale=gain[:, t : t + 1]
+                )
+            drift = ring.tile([P, D * P], F32, name="drift")
+            nc.vector.tensor_tensor(drift[:], st["dst_t"][:], prexp[:], ALU.mult)
+            pair_product = ring.tile([P, P // 2], F32, name="pair_product")
+            nc.vector.tensor_tensor(pair_product[:], exp_sum[:, : P // 2], upper[:], ALU.mult)
+            add_up(drift_sum, drift)
+            inv_pair = ring.tile([P, P // 2], F32, name="inv_pair")
+            nc.vector.reciprocal(inv_pair[:], pair_product[:])
+            st.update(drift_sum=drift_sum, partner=partner, inv_pair=inv_pair)
+
+        def total(c):
+            st = stages[c]
+            drift_sum, partner, inv_pair = st["drift_sum"], st["partner"], st["inv_pair"]
+            crossed = ring.tile([P, 2, P // 2], F32, name="crossed")
+            nc.vector.tensor_tensor(
+                crossed[:].rearrange("p a g -> p (a g)"), drift_sum, partner[:].rearrange("p t g -> p (t g)"), ALU.mult
+            )
+            tot = ring.tile([P, P], F32, name="tot")
+            nc.vector.tensor_tensor(
+                tot[:].rearrange("p (a g) -> p a g", a=2),
+                crossed[:],
+                inv_pair[:].unsqueeze(1).to_broadcast([P, 2, P // 2]),
+                ALU.mult,
+            )
+            st["tot"] = tot
+
+        def programme(c):
+            st = stages[c]
+            hid = ring.tile([P, CW * PACK], BF16, name="hid", align_bytes=64)
+            nc.vector.tensor_tensor(
+                hid[:].rearrange("p (g d t) -> p g t d", d=D, t=PACK),
+                vel[:, c].rearrange("p t (g d) -> p g t d", d=D),
+                st["tot"][:].rearrange("p (t g) -> p g t", t=PACK).unsqueeze(3).to_broadcast([P, GROUPS, PACK, D]),
+                ALU.mult,
+            )
+            codes = ring.tile([P, CW], U32, name="codes", align_bytes=64)
+            plane = ring.tile([P, CW], U8, name="plane", align_bytes=64)
+            nc.vector.quantize_mx(out=codes[:].bitcast(FP8X4), scales=plane[:], in_=hid[:])
+            acc = bank(c)
+            for h in range(N // P):
+                nc.tensor.matmul_mx(
+                    out=acc[:, CW * h : CW * (h + 1)],
+                    lhsT=w3_sb[:, 2 * P * h : 2 * P * (h + 1)].bitcast(FP4X4),
+                    lhsT_scale=w3_plane[:, P * h : P * (h + 1)],
+                    rhs=codes[:].bitcast(FP8X4),
+                    rhs_scale=plane[:],
+                    start=True,
+                    stop=True,
+                )
+            result = ring.tile([P, N // P * CW], F32, name="result")
+            nc.scalar.copy(result[:], acc[:, : N // P * CW])
+            nc.sync.dma_start(
+                out=out[:, CW * c : CW * (c + 1)].rearrange("(h p) j -> p h j", p=P),
+                in_=result[:].rearrange("p (h j) -> p h j", j=CW),
+            )
+
+        stage_lag = ((cosine, 0), (weights, 1), (total, 2), (programme, 3))
+        for step in range(CHUNKS + 3):
+            for stage, lag in stage_lag:
+                if 0 <= step - lag < CHUNKS:
+                    stage(step - lag)

@@ -136,15 +136,19 @@ def tile_picked_yrnavl_tot_p_kernel(
         for t in range(PACK):
             nc.scalar.activation(sig_sp[t][:], sp[t][:], ACT.Sigmoid, scale=-1.0)
             window = keep.tile([P, S], F32, name="window%d" % t)
-            nc.scalar.copy(window[:], sp[t][:])
+            if t in (2, 3):
+                nc.vector.tensor_copy(window[:], sp[t][:])
+            else:
+                nc.scalar.copy(window[:], sp[t][:])
             fetched = ring.tile([P, S], F32, name="fetched")
             for h in range(2):
                 nc.vector.tensor_copy(fetched[:, 256 * h : 256 * (h + 1)], window[:].indirect(nei_sb[:, 16 * h : 16 * (h + 1)]))
-            nc.vector.tensor_tensor(dst[:, :, t, :], by_chunk(fetched[:]), by_chunk(window[:]), ALU.subtract)
-            if t in (0,):
-                nc.vector.scalar_tensor_tensor(abs_dst[:, :, t, :], dst[:, :, t, :], -1.0, dst[:, :, t, :], ALU.mult, ALU.max)
+            nc.gpsimd.tensor_tensor(dst[:, :, t, :], by_chunk(fetched[:]), by_chunk(window[:]), ALU.subtract)
         for t in range(PACK):
             nc.scalar.activation(sig_un[t][:], un[t][:], ACT.Sigmoid, scale=-1.0)
+
+        for t in (0,):
+            nc.vector.scalar_tensor_tensor(abs_dst[:, :, t, :], dst[:, :, t, :], -1.0, dst[:, :, t, :], ALU.mult, ALU.max)
 
         vel = wide("vel")
         log_den = wide("log_den")
@@ -171,9 +175,15 @@ def tile_picked_yrnavl_tot_p_kernel(
         def flat(ap):
             return ap.rearrange("p t j -> p (t j)")
 
+        def grouped(ap):
+            return ap.rearrange("p (g d) -> p g d", d=D)
+
+        def member_major(ap):
+            return ap.rearrange("p (d g) -> p g d", d=D)
+
         num = wide("num")
         for c in range(CHUNKS):
-            nc.vector.tensor_tensor(flat(num[:, c]), flat(vel[:, c]), flat(dst[:, c]), ALU.mult)
+            nc.vector.tensor_tensor(member_major(flat(num[:, c])), grouped(flat(vel[:, c])), grouped(flat(dst[:, c])), ALU.mult)
 
         stages = [dict() for c in range(CHUNKS)]
         for c in range(CHUNKS):
@@ -185,17 +195,17 @@ def tile_picked_yrnavl_tot_p_kernel(
         def cosine(c):
             st = stages[c]
             inv_den = ring.tile([P, PACK * CW], F32, name="inv_den")
-            nc.scalar.activation(inv_den[:], flat(log_den[:, c]), ACT.Exp, scale=-1.0)
+            nc.scalar.activation(member_major(inv_den[:]), grouped(flat(log_den[:, c])), ACT.Exp, scale=-1.0)
             cosn = ring.tile([P, PACK * CW], F32, name="cosn")
             nc.vector.tensor_tensor(cosn[:], flat(num[:, c]), inv_den[:], ALU.mult)
             neg_top = ring.tile([P, P], F32, name="neg_top")
             nc.vector.tensor_reduce(
-                neg_top[:], cosn[:].rearrange("p (g d) -> p g d", d=D), mybir.AxisListType.X, ALU.max, negate=True
+                neg_top[:], member_major(cosn[:]), mybir.AxisListType.X, ALU.max, negate=True
             )
             shifted = bank(4 + c % 2)
             for d in range(D):
                 nc.tensor.matmul(
-                    shifted[:, P * d : P * (d + 1)], cosn[:, d :: D], ident[:], start=(d == 0), stop=False, is_transpose=True
+                    shifted[:, P * d : P * (d + 1)], cosn[:, P * d : P * (d + 1)], ident[:], start=(d == 0), stop=False, is_transpose=True
                 )
             for d in range(D):
                 nc.tensor.matmul(

@@ -157,20 +157,27 @@ def tile_picked_yrnavl_tot_p_kernel(
             log_un = ring.tile([P, S], F32, name="log_un")
             nc.scalar.activation(log_sp[:], sig_sp[t][:], ACT.Ln, bias=LN_FLOOR)
             nc.scalar.activation(log_un[:], sig_un[t][:], ACT.Ln, bias=LN_FLOOR)
-            soft_sp = ring.tile([P, S], F32, name="soft_sp")
-            soft_un = ring.tile([P, S], F32, name="soft_un")
-            nc.vector.scalar_tensor_tensor(soft_sp[:], sp[t][:], -1.0, log_sp[:], ALU.mult, ALU.min)
-            nc.vector.scalar_tensor_tensor(soft_un[:], un[t][:], -1.0, log_un[:], ALU.mult, ALU.min)
-            nc.vector.scalar_tensor_tensor(
-                vel[:, :, t, :], by_chunk(soft_un[:]), rate[:, t : t + 1], by_chunk(soft_sp[:]), ALU.mult, ALU.add
-            )
-            abs_vel = ring.tile([P, S], F32, name="abs_vel")
             if t not in (0,):
                 nc.scalar.activation(abs_dst[:, :, t, :], dst[:, :, t, :], ACT.Abs)
-            nc.scalar.activation(by_chunk(abs_vel[:]), vel[:, :, t, :], ACT.Abs, scale=DECAY)
-            den = ring.tile([P, S], F32, name="den")
-            nc.vector.tensor_tensor(by_chunk(den[:]), by_chunk(abs_vel[:]), abs_dst[:, :, t, :], ALU.add)
-            nc.scalar.activation(log_den[:, :, t, :], by_chunk(den[:]), ACT.Ln, bias=DEN_BIAS)
+            step = CHUNKS if t < PACK - 1 else 2
+            for first in range(0, CHUNKS, step):
+                chunks = slice(first, first + step)
+                soft_sp = ring.tile([P, step, CW], F32, name="soft_sp")
+                soft_un = ring.tile([P, step, CW], F32, name="soft_un")
+                nc.vector.scalar_tensor_tensor(
+                    soft_sp[:], by_chunk(sp[t][:])[:, chunks], -1.0, by_chunk(log_sp[:])[:, chunks], ALU.mult, ALU.min
+                )
+                nc.vector.scalar_tensor_tensor(
+                    soft_un[:], by_chunk(un[t][:])[:, chunks], -1.0, by_chunk(log_un[:])[:, chunks], ALU.mult, ALU.min
+                )
+                nc.vector.scalar_tensor_tensor(
+                    vel[:, chunks, t, :], soft_un[:], rate[:, t : t + 1], soft_sp[:], ALU.mult, ALU.add
+                )
+                abs_vel = ring.tile([P, step, CW], F32, name="abs_vel")
+                nc.scalar.activation(abs_vel[:], vel[:, chunks, t, :], ACT.Abs, scale=DECAY)
+                den = ring.tile([P, step, CW], F32, name="den")
+                nc.vector.tensor_tensor(den[:], abs_vel[:], abs_dst[:, chunks, t, :], ALU.add)
+                nc.scalar.activation(log_den[:, chunks, t, :], den[:], ACT.Ln, bias=DEN_BIAS)
 
         def flat(ap):
             return ap.rearrange("p t j -> p (t j)")
@@ -181,7 +188,7 @@ def tile_picked_yrnavl_tot_p_kernel(
         def member_major(ap):
             return ap.rearrange("p (d g) -> p g d", d=D)
 
-        num = wide("num")
+        num = abs_dst
         for c in range(CHUNKS):
             nc.vector.tensor_tensor(member_major(flat(num[:, c])), grouped(flat(vel[:, c])), grouped(flat(dst[:, c])), ALU.mult)
 
@@ -197,7 +204,7 @@ def tile_picked_yrnavl_tot_p_kernel(
             inv_den = ring.tile([P, PACK * CW], F32, name="inv_den")
             nc.scalar.activation(member_major(inv_den[:]), grouped(flat(log_den[:, c])), ACT.Exp, scale=-1.0)
             cosn = ring.tile([P, PACK * CW], F32, name="cosn")
-            nc.vector.tensor_tensor(cosn[:], flat(num[:, c]), inv_den[:], ALU.mult)
+            (nc.gpsimd if c in (1, 2, 3) else nc.vector).tensor_tensor(cosn[:], flat(num[:, c]), inv_den[:], ALU.mult)
             neg_top = ring.tile([P, P], F32, name="neg_top")
             nc.vector.tensor_reduce(
                 neg_top[:], member_major(cosn[:]), mybir.AxisListType.X, ALU.max, negate=True
@@ -217,9 +224,7 @@ def tile_picked_yrnavl_tot_p_kernel(
             st = stages[c]
             prexp = ring.tile([P, D * P], F32, name="prexp")
             nc.scalar.activation(prexp[:], st["shifted"][:], ACT.Exp, scale=DECAY)
-            sums = bank(6 + c % 2)
-            exp_sum = sums[:, :P]
-            drift_sum = sums[:, P : 2 * P]
+            exp_sum = bank(6 + c % 2)[:, :P]
 
             def add_up(total, terms):
                 for d in range(D):
@@ -240,6 +245,7 @@ def tile_picked_yrnavl_tot_p_kernel(
             nc.vector.tensor_tensor(drift[:], st["dst_t"][:], prexp[:], ALU.mult)
             pair_product = ring.tile([P, P // 2], F32, name="pair_product")
             nc.vector.tensor_tensor(pair_product[:], exp_sum[:, : P // 2], upper[:], ALU.mult)
+            drift_sum = bank(c)[:, :P]
             add_up(drift_sum, drift)
             inv_pair = ring.tile([P, P // 2], F32, name="inv_pair")
             nc.vector.reciprocal(inv_pair[:], pair_product[:])
@@ -273,10 +279,10 @@ def tile_picked_yrnavl_tot_p_kernel(
             codes = ring.tile([P, CW], U32, name="codes", align_bytes=64)
             plane = ring.tile([P, CW], U8, name="plane", align_bytes=64)
             nc.vector.quantize_mx(out=codes[:].bitcast(FP8X4), scales=plane[:], in_=hid[:])
-            acc = bank(c)
             for h in range(N // P):
+                acc = bank(c if h == 0 else 4 + c % 2)[:, :CW]
                 nc.tensor.matmul_mx(
-                    out=acc[:, CW * h : CW * (h + 1)],
+                    out=acc,
                     lhsT=w3_sb[:, 2 * P * h : 2 * P * (h + 1)].bitcast(FP4X4),
                     lhsT_scale=w3_plane[:, P * h : P * (h + 1)],
                     rhs=codes[:].bitcast(FP8X4),
@@ -284,12 +290,12 @@ def tile_picked_yrnavl_tot_p_kernel(
                     start=True,
                     stop=True,
                 )
-            result = ring.tile([P, N // P * CW], F32, name="result")
-            nc.scalar.copy(result[:], acc[:, : N // P * CW])
-            nc.sync.dma_start(
-                out=out[:, CW * c : CW * (c + 1)].rearrange("(h p) j -> p h j", p=P),
-                in_=result[:].rearrange("p (h j) -> p h j", j=CW),
-            )
+                result = ring.tile([P, CW], F32, name="result")
+                if h == 1 and c == CHUNKS - 1:
+                    nc.vector.tensor_copy(result[:], acc)
+                else:
+                    nc.scalar.copy(result[:], acc)
+                (nc.sync if h == 0 or c < CHUNKS - 1 else nc.scalar).dma_start(out=out[P * h : P * (h + 1), CW * c : CW * (c + 1)], in_=result[:])
 
         stage_lag = ((cosine, 0), (weights, 1), (total, 2), (programme, 3))
         for step in range(CHUNKS + 3):

@@ -159,25 +159,25 @@ def tile_picked_yrnavl_tot_p_kernel(
             nc.scalar.activation(log_un[:], sig_un[t][:], ACT.Ln, bias=LN_FLOOR)
             if t not in (0,):
                 nc.scalar.activation(abs_dst[:, :, t, :], dst[:, :, t, :], ACT.Abs)
-            step = CHUNKS if t < PACK - 1 else 2
-            for first in range(0, CHUNKS, step):
-                chunks = slice(first, first + step)
-                soft_sp = ring.tile([P, step, CW], F32, name="soft_sp")
-                soft_un = ring.tile([P, step, CW], F32, name="soft_un")
+            width = CW if t < PACK - 1 else CW // 2
+            for first in range(0, CW, width):
+                cols = slice(first, first + width)
+                soft_sp = ring.tile([P, CHUNKS, width], F32, name="soft_sp")
+                soft_un = ring.tile([P, CHUNKS, width], F32, name="soft_un")
                 nc.vector.scalar_tensor_tensor(
-                    soft_sp[:], by_chunk(sp[t][:])[:, chunks], -1.0, by_chunk(log_sp[:])[:, chunks], ALU.mult, ALU.min
+                    soft_sp[:], by_chunk(sp[t][:])[:, :, cols], -1.0, by_chunk(log_sp[:])[:, :, cols], ALU.mult, ALU.min
                 )
                 nc.vector.scalar_tensor_tensor(
-                    soft_un[:], by_chunk(un[t][:])[:, chunks], -1.0, by_chunk(log_un[:])[:, chunks], ALU.mult, ALU.min
+                    soft_un[:], by_chunk(un[t][:])[:, :, cols], -1.0, by_chunk(log_un[:])[:, :, cols], ALU.mult, ALU.min
                 )
                 nc.vector.scalar_tensor_tensor(
-                    vel[:, chunks, t, :], soft_un[:], rate[:, t : t + 1], soft_sp[:], ALU.mult, ALU.add
+                    vel[:, :, t, cols], soft_un[:], rate[:, t : t + 1], soft_sp[:], ALU.mult, ALU.add
                 )
-                abs_vel = ring.tile([P, step, CW], F32, name="abs_vel")
-                nc.scalar.activation(abs_vel[:], vel[:, chunks, t, :], ACT.Abs, scale=DECAY)
-                den = ring.tile([P, step, CW], F32, name="den")
-                nc.vector.tensor_tensor(den[:], abs_vel[:], abs_dst[:, chunks, t, :], ALU.add)
-                nc.scalar.activation(log_den[:, chunks, t, :], den[:], ACT.Ln, bias=DEN_BIAS)
+                abs_vel = ring.tile([P, CHUNKS, width], F32, name="abs_vel")
+                nc.scalar.activation(abs_vel[:], vel[:, :, t, cols], ACT.Abs, scale=DECAY)
+                den = ring.tile([P, CHUNKS, width], F32, name="den")
+                nc.vector.tensor_tensor(den[:], abs_vel[:], abs_dst[:, :, t, cols], ALU.add)
+                nc.scalar.activation(log_den[:, :, t, cols], den[:], ACT.Ln, bias=DEN_BIAS)
 
         def flat(ap):
             return ap.rearrange("p t j -> p (t j)")
@@ -204,7 +204,7 @@ def tile_picked_yrnavl_tot_p_kernel(
             inv_den = ring.tile([P, PACK * CW], F32, name="inv_den")
             nc.scalar.activation(member_major(inv_den[:]), grouped(flat(log_den[:, c])), ACT.Exp, scale=-1.0)
             cosn = ring.tile([P, PACK * CW], F32, name="cosn")
-            (nc.gpsimd if c in (1, 2, 3) else nc.vector).tensor_tensor(cosn[:], flat(num[:, c]), inv_den[:], ALU.mult)
+            nc.vector.tensor_tensor(cosn[:], flat(num[:, c]), inv_den[:], ALU.mult)
             neg_top = ring.tile([P, P], F32, name="neg_top")
             nc.vector.tensor_reduce(
                 neg_top[:], member_major(cosn[:]), mybir.AxisListType.X, ALU.max, negate=True

from contextlib import ExitStack

import concourse.mybir as mybir
from concourse.masks import make_identity

K, T, S, D, N, H = 512, 2048, 512, 4, 256, 512
FLOPS = 2 * K * H * S * 2 + 2 * H * N * S

F32 = mybir.dt.float32
BF16 = mybir.dt.bfloat16
I32 = mybir.dt.int32
U32 = mybir.dt.uint32
U16 = mybir.dt.uint16
U8 = mybir.dt.uint8
FP8X4 = mybir.dt.float8_e4m3fn_x4
FP4X4 = mybir.dt.float4_e2m1fn_x4
ALU = mybir.AluOpType
ACT = mybir.ActivationFunctionType

P = 128
PACK = 4
CHUNKS = 4
CW = S // CHUNKS
GROUPS = CW // D
DECAY = 0.7
DEN_BIAS = 0.3
LN_FLOOR = 2.0**-64


def load_scale_rows(queues, plane, scales):
    for q, queue in enumerate(queues):
        queue.dma_start(out=plane[32 * q : 32 * q + 4, :].bitcast(I32), in_=scales[0, 4 * q : 4 * q + 4, :].bitcast(I32))


def deal_columns(nc, pool, name, words, plane):
    dealt_words = pool.tile([P, 2 * H], U8, name=name + "_dealt_words", align_bytes=64)
    dealt_plane = pool.tile([P, H], U8, name=name + "_dealt_plane", align_bytes=64)
    nc.vector.tensor_copy(
        out=dealt_words[:].rearrange("p (t a m b) -> p a t m b", t=PACK, m=8, b=2),
        in_=words[:].rearrange("p (a m t b) -> p a t m b", t=PACK, m=8, b=2),
    )
    nc.vector.tensor_copy(
        out=dealt_plane[:].rearrange("p (t a m) -> p a t m", t=PACK, m=16),
        in_=plane[:].rearrange("p (a m t) -> p a t m", t=PACK, m=16),
    )
    return dealt_words, dealt_plane


def tile_picked_yrnavl_tot_p_kernel(
    tc, x_words, x_scales, w1_words, w1_scales, w2_words, w2_scales, beta, unit, w3_words, w3_scales, offs, nei, out
):
    nc = tc.nc
    with ExitStack() as ctx:
        keep = ctx.enter_context(tc.tile_pool(name="keep", bufs=1))
        ring = ctx.enter_context(tc.tile_pool(name="ring", bufs=4))
        psum = ctx.enter_context(tc.psum_pool(name="psum", bufs=1))

        def bank(b):
            return psum.tile([P, 512], F32, name="bank%d" % b, tag="bank%d" % b)

        x_plane = keep.tile([P, T], U8, name="x_plane", tag="x_plane", align_bytes=64)
        w_plane = keep.tile([P, H], U8, name="w_plane", align_bytes=64)
        w1_plane = keep.tile([P, H], U8, name="w1_plane", align_bytes=64)
        nc.gpsimd.memset(x_plane[:].bitcast(I32), 0)
        nc.gpsimd.memset(w_plane[:].bitcast(I32), 0)
        nc.gpsimd.memset(w1_plane[:].bitcast(I32), 0)

        x_table = keep.tile([P, T], I32, name="x_table", tag="x_table", align_bytes=64)
        offs_sb = keep.tile([P, S // 16], U16, name="offs_sb")
        nei_sb = keep.tile([P, S // 16], U16, name="nei_sb")
        w_words = keep.tile([P, 2 * H], U8, name="w_words", align_bytes=64)
        on_sync = [nc.sync] * 4

        nc.sync.dma_start(offs_sb[:], offs)
        nc.sync.dma_start(out=w_words[:].bitcast(I32), in_=w2_words[0].bitcast(I32))
        load_scale_rows(on_sync, x_plane, x_scales)
        nc.sync.dma_start(out=x_table[:], in_=x_words[0].rearrange("p n t -> p (n t)").bitcast(I32))
        load_scale_rows([nc.sync, nc.sync, nc.sync, nc.gpsimd], w_plane, w2_scales)

        ident = keep.tile([P, P], F32, name="ident")
        make_identity(nc, ident[:])

        x_codes = keep.tile([P, S], U32, name="x_codes", align_bytes=64)
        x_picked_plane = keep.tile([P, S], U8, name="x_picked_plane", align_bytes=64)
        w2_dealt, w2_dealt_plane = deal_columns(nc, keep, "w2", w_words, w_plane)
        nc.vector.tensor_copy(x_picked_plane[:], x_plane[:].indirect(offs_sb[:]))
        nc.vector.tensor_copy(x_codes[:], x_table[:].bitcast(U32).indirect(offs_sb[:]))

        nc.sync.dma_start(out=w_words[:].bitcast(I32), in_=w1_words[0].bitcast(I32))
        load_scale_rows(on_sync, w1_plane, w1_scales)
        nc.sync.dma_start(nei_sb[:], nei)
        w1_dealt, w1_dealt_plane = deal_columns(nc, keep, "w1", w_words, w1_plane)

        beta_sb = keep.tile([P, PACK], F32, name="beta_sb", tag="x_table", align_bytes=64)
        unit_sb = keep.tile([P, PACK], F32, name="unit_sb", tag="x_plane", align_bytes=64)
        nc.sync.dma_start(out=beta_sb[:], in_=beta.rearrange("(p t) o -> p (t o)", t=PACK))
        nc.sync.dma_start(out=unit_sb[:], in_=unit.rearrange("(p t) o -> p (t o)", t=PACK))
        w3_sb = w_words[:, : 2 * N]
        w3_plane = w_plane[:, :N]
        nc.sync.dma_start(out=w3_sb.bitcast(I32), in_=w3_words[0].bitcast(I32))
        load_scale_rows(on_sync, w3_plane, w3_scales)

        rate = keep.tile([P, PACK], F32, name="rate")
        gain = keep.tile([P, PACK], F32, name="gain")
        nc.gpsimd.tensor_scalar(rate[:], beta_sb[:], -1.0 / DECAY, 0.0, ALU.mult, ALU.add)
        nc.gpsimd.tensor_scalar(gain[:], unit_sb[:], DECAY, 0.0, ALU.mult, ALU.add)

        def product(acc, words, plane, t):
            nc.tensor.matmul_mx(
                out=acc[:],
                lhsT=words[:, 2 * P * t : 2 * P * (t + 1)].bitcast(FP4X4),
                lhsT_scale=plane[:, P * t : P * (t + 1)],
                rhs=x_codes[:].bitcast(FP8X4),
                rhs_scale=x_picked_plane[:],
                start=True,
                stop=True,
            )

        def wide(name):
            return keep.tile([P, CHUNKS, PACK, CW], F32, name=name)

        def by_chunk(ap):
            return ap.rearrange("p (c j) -> p c j", c=CHUNKS)

        sp = [bank(t) for t in range(PACK)]
        un = [bank(PACK + t) for t in range(PACK)]
        for t in range(PACK):
            product(sp[t], w2_dealt, w2_dealt_plane, t)
        for t in range(PACK):
            product(un[t], w1_dealt, w1_dealt_plane, t)

        dst = wide("dst")
        abs_dst = wide("abs_dst")
        sig_sp = [keep.tile([P, S], F32, name="sig_sp%d" % t) for t in range(PACK)]
        sig_un = [keep.tile([P, S], F32, name="sig_un%d" % t) for t in range(PACK)]
        for t in range(PACK):
            nc.scalar.activation(sig_sp[t][:], sp[t][:], ACT.Sigmoid, scale=-1.0)
            window = keep.tile([P, S], F32, name="window%d" % t)
            if t in (2, 3):
                nc.vector.tensor_copy(window[:], sp[t][:])
            else:
                nc.scalar.copy(window[:], sp[t][:])
            fetched = ring.tile([P, S], F32, name="fetched")
            for h in range(2):
                nc.vector.tensor_copy(fetched[:, 256 * h : 256 * (h + 1)], window[:].indirect(nei_sb[:, 16 * h : 16 * (h + 1)]))
            nc.gpsimd.tensor_tensor(dst[:, :, t, :], by_chunk(fetched[:]), by_chunk(window[:]), ALU.subtract)
        for t in range(PACK):
            nc.scalar.activation(sig_un[t][:], un[t][:], ACT.Sigmoid, scale=-1.0)

        for t in (0,):
            nc.vector.scalar_tensor_tensor(abs_dst[:, :, t, :], dst[:, :, t, :], -1.0, dst[:, :, t, :], ALU.mult, ALU.max)

        vel = wide("vel")
        log_den = wide("log_den")
        for t in range(PACK):
            log_sp = ring.tile([P, S], F32, name="log_sp")
            log_un = ring.tile([P, S], F32, name="log_un")
            nc.scalar.activation(log_sp[:], sig_sp[t][:], ACT.Ln, bias=LN_FLOOR)
            nc.scalar.activation(log_un[:], sig_un[t][:], ACT.Ln, bias=LN_FLOOR)
            if t not in (0,):
                nc.scalar.activation(abs_dst[:, :, t, :], dst[:, :, t, :], ACT.Abs)
            width = CW if t < PACK - 1 else CW // 2
            for first in range(0, CW, width):
                cols = slice(first, first + width)
                soft_sp = ring.tile([P, CHUNKS, width], F32, name="soft_sp")
                soft_un = ring.tile([P, CHUNKS, width], F32, name="soft_un")
                nc.vector.scalar_tensor_tensor(
                    soft_sp[:], by_chunk(sp[t][:])[:, :, cols], -1.0, by_chunk(log_sp[:])[:, :, cols], ALU.mult, ALU.min
                )
                nc.vector.scalar_tensor_tensor(
                    soft_un[:], by_chunk(un[t][:])[:, :, cols], -1.0, by_chunk(log_un[:])[:, :, cols], ALU.mult, ALU.min
                )
                nc.vector.scalar_tensor_tensor(
                    vel[:, :, t, cols], soft_un[:], rate[:, t : t + 1], soft_sp[:], ALU.mult, ALU.add
                )
                abs_vel = ring.tile([P, CHUNKS, width], F32, name="abs_vel")
                nc.scalar.activation(abs_vel[:], vel[:, :, t, cols], ACT.Abs, scale=DECAY)
                den = ring.tile([P, CHUNKS, width], F32, name="den")
                nc.vector.tensor_tensor(den[:], abs_vel[:], abs_dst[:, :, t, cols], ALU.add)
                nc.scalar.activation(log_den[:, :, t, cols], den[:], ACT.Ln, bias=DEN_BIAS)

        def flat(ap):
            return ap.rearrange("p t j -> p (t j)")

        def grouped(ap):
            return ap.rearrange("p (g d) -> p g d", d=D)

        def member_major(ap):
            return ap.rearrange("p (d g) -> p g d", d=D)

        num = abs_dst
        for c in range(CHUNKS):
            nc.vector.tensor_tensor(member_major(flat(num[:, c])), grouped(flat(vel[:, c])), grouped(flat(dst[:, c])), ALU.mult)

        stages = [dict() for c in range(CHUNKS)]
        for c in range(CHUNKS):
            dst_t = bank(c)
            for d in range(D):
                nc.tensor.transpose(dst_t[:, P * d : P * (d + 1)], flat(dst[:, c])[:, d :: D], ident[:])
            stages[c]["dst_t"] = dst_t

        def cosine(c):
            st = stages[c]
            inv_den = ring.tile([P, PACK * CW], F32, name="inv_den")
            nc.scalar.activation(member_major(inv_den[:]), grouped(flat(log_den[:, c])), ACT.Exp, scale=-1.0)
            cosn = ring.tile([P, PACK * CW], F32, name="cosn")
            nc.vector.tensor_tensor(cosn[:], flat(num[:, c]), inv_den[:], ALU.mult)
            neg_top = ring.tile([P, P], F32, name="neg_top")
            nc.vector.tensor_reduce(
                neg_top[:], member_major(cosn[:]), mybir.AxisListType.X, ALU.max, negate=True
            )
            shifted = bank(4 + c % 2)
            for d in range(D):
                nc.tensor.matmul(
                    shifted[:, P * d : P * (d + 1)], cosn[:, P * d : P * (d + 1)], ident[:], start=(d == 0), stop=False, is_transpose=True
                )
            for d in range(D):
                nc.tensor.matmul(
                    shifted[:, P * d : P * (d + 1)], neg_top[:], ident[:], start=False, stop=(d == D - 1), is_transpose=True
                )
            st["shifted"] = shifted

        def weights(c):
            st = stages[c]
            prexp = ring.tile([P, D * P], F32, name="prexp")
            nc.scalar.activation(prexp[:], st["shifted"][:], ACT.Exp, scale=DECAY)
            exp_sum = bank(6 + c % 2)[:, :P]

            def add_up(total, terms):
                for d in range(D):
                    nc.tensor.matmul(
                        total, terms[:, P * d : P * (d + 1)], ident[:], start=(d == 0), stop=(d == D - 1), is_transpose=True
                    )

            add_up(exp_sum, prexp)
            upper = ring.tile([P, P // 2], F32, name="upper")
            nc.scalar.copy(upper[:], exp_sum[:, P // 2 :])
            partner = ring.tile([P, PACK, GROUPS], F32, name="partner")
            for t in range(PACK):
                other = (t + 2) % PACK
                nc.scalar.activation(
                    partner[:, t, :], exp_sum[:, GROUPS * other : GROUPS * (other + 1)], ACT.Copy, scale=gain[:, t : t + 1]
                )
            drift = ring.tile([P, D * P], F32, name="drift")
            nc.vector.tensor_tensor(drift[:], st["dst_t"][:], prexp[:], ALU.mult)
            pair_product = ring.tile([P, P // 2], F32, name="pair_product")
            nc.vector.tensor_tensor(pair_product[:], exp_sum[:, : P // 2], upper[:], ALU.mult)
            drift_sum = bank(c)[:, :P]
            add_up(drift_sum, drift)
            inv_pair = ring.tile([P, P // 2], F32, name="inv_pair")
            nc.vector.reciprocal(inv_pair[:], pair_product[:])
            st.update(drift_sum=drift_sum, partner=partner, inv_pair=inv_pair)

        def total(c):
            st = stages[c]
            drift_sum, partner, inv_pair = st["drift_sum"], st["partner"], st["inv_pair"]
            crossed = ring.tile([P, 2, P // 2], F32, name="crossed")
            nc.vector.tensor_tensor(
                crossed[:].rearrange("p a g -> p (a g)"), drift_sum, partner[:].rearrange("p t g -> p (t g)"), ALU.mult
            )
            tot = ring.tile([P, P], F32, name="tot")
            nc.vector.tensor_tensor(
                tot[:].rearrange("p (a g) -> p a g", a=2),
                crossed[:],
                inv_pair[:].unsqueeze(1).to_broadcast([P, 2, P // 2]),
                ALU.mult,
            )
            st["tot"] = tot

        def programme(c):
            st = stages[c]
            hid = ring.tile([P, CW * PACK], BF16, name="hid", align_bytes=64)
            nc.vector.tensor_tensor(
                hid[:].rearrange("p (g d t) -> p g t d", d=D, t=PACK),
                vel[:, c].rearrange("p t (g d) -> p g t d", d=D),
                st["tot"][:].rearrange("p (t g) -> p g t", t=PACK).unsqueeze(3).to_broadcast([P, GROUPS, PACK, D]),
                ALU.mult,
            )
            codes = ring.tile([P, CW], U32, name="codes", align_bytes=64)
            plane = ring.tile([P, CW], U8, name="plane", align_bytes=64)
            nc.vector.quantize_mx(out=codes[:].bitcast(FP8X4), scales=plane[:], in_=hid[:])
            for h in range(N // P):
                acc = bank(c if h == 0 else 4 + c % 2)[:, :CW]
                nc.tensor.matmul_mx(
                    out=acc,
                    lhsT=w3_sb[:, 2 * P * h : 2 * P * (h + 1)].bitcast(FP4X4),
                    lhsT_scale=w3_plane[:, P * h : P * (h + 1)],
                    rhs=codes[:].bitcast(FP8X4),
                    rhs_scale=plane[:],
                    start=True,
                    stop=True,
                )
                result = ring.tile([P, CW], F32, name="result")
                if h == 1 and c == CHUNKS - 1:
                    nc.vector.tensor_copy(result[:], acc)
                else:
                    nc.scalar.copy(result[:], acc)
                (nc.sync if h == 0 or c < CHUNKS - 1 else nc.scalar).dma_start(out=out[P * h : P * (h + 1), CW * c : CW * (c + 1)], in_=result[:])

        stage_lag = ((cosine, 0), (weights, 1), (total, 2), (programme, 3))
        for step in range(CHUNKS + 3):
            for stage, lag in stage_lag:
                if 0 <= step - lag < CHUNKS:
                    stage(step - lag)
